import numpy as np, ml_dtypes
CORES = [2,3,42,43,82,83,122,123]
N = 8
import mx_ref
BF = ml_dtypes.bfloat16
def entries(a):
    return np.ascontiguousarray(a.T).reshape(-1)
def table(e):
    return np.ascontiguousarray(np.reshape(e, (-1, 16)).T).astype(np.int32)
def cols(t, e):
    v = np.concatenate([t.reshape(128, -1, 4), np.zeros((128, 1, 4), BF)], axis=1)
    return np.ascontiguousarray(v[:, e]).reshape(128, -1)
def f(rng, *shape):
    return mx_ref.flush((rng.standard_normal(shape, dtype=np.float32) * np.exp2(rng.integers(-2, 3, shape[:-1] + (1,)))).astype(BF))
def wide(rng, *shape, cols=0):
    v = rng.standard_normal(shape, dtype=np.float32) * np.exp2(rng.integers(-12, 13, shape)).astype(np.float32)
    if cols: v *= np.repeat(np.exp2(rng.integers(-cols, cols + 1, shape[:-2] + (1, shape[-1] // 4))) * (rng.random(shape[:-2] + (1, shape[-1] // 4)) > 0.0625), 4, axis=-1).astype(np.float32)
    return mx_ref.flush(v.astype(BF))
T, S, CAPP = 512, 256, 48
def lists(rng, most=None, own=False, share=False, edge=False):
    o, c, m = [], [], []
    for r in range(N):
        n = np.zeros(N, int)
        if own: n[r] = CAPP
        if most is not None:
            for q in rng.permutation(N)[:most]: n[q] = CAPP
            n = np.minimum(n, np.maximum(0, S - (np.cumsum(n) - n)))
        while n.sum() < S:
            q = rng.integers(0, N)
            if n[q] < CAPP: n[q] += 1
        slots = np.full(N * CAPP, -1); used = []
        for q in range(N):
            k = q * CAPP + rng.permutation(CAPP)[:n[q]]; used += list(k)
            slots[k] = rng.integers(0, T) if share else rng.choice([0, T - 1], n[q]) if edge else rng.integers(0, T, n[q])
        o.append(table(rng.choice([0, T - 1], S) if edge else rng.integers(0, T, S))); c.append(table(slots)); m.append(table(rng.permutation(used)))
    return {"own": np.stack(o), "want": np.stack(c), "slot": np.stack(m)}
def setup_inputs(rng):
    return {"x": f(rng, N, 128, 4 * T), "w": f(rng, N, 128, 512), **lists(rng)}
def setup_inputs_edge(rng):
    return {**setup_inputs(rng), **lists(rng, edge=True)}
def setup_inputs_full(rng):
    return {**setup_inputs(rng), **lists(rng, most=S // CAPP)}
def setup_inputs_self(rng):
    return {**setup_inputs(rng), **lists(rng, own=True)}
def setup_inputs_share(rng):
    return {**setup_inputs(rng), **lists(rng, share=True)}
def setup_inputs_spread(rng):
    d = setup_inputs(rng); d["x"] = wide(rng, N, 128, 4 * T, cols=8); return d
def check_inputs(d):
    b = []
    for r in range(N):
        o, c, m = entries(d["own"][r]), entries(d["want"][r]), entries(d["slot"][r])
        if o.min() < 0 or o.max() >= T: b.append("own")
        if c.min() < -1 or c.max() >= T: b.append("want")
        if m.min() < 0 or m.max() >= N * CAPP or len(set(m.tolist())) != S or (c[m] < 0).any() or (c >= 0).sum() != S: b.append("slot")
    return b
def decode(q):
    out = np.zeros(q[0].shape, np.float32)
    for b in range(4):
        e = np.zeros((128, 128, 4), np.float32); e[np.arange(128), np.arange(128), b] = 1
        out[:, b::4] = mx_ref.matmul(mx_ref.quantize(e.reshape(128, 512).astype(BF)), q)
    return out
def reference(x, w, own, want, slot):
    M = []
    for r in range(N):
        c = entries(want[r])
        arrived = np.concatenate([decode(mx_ref.quantize(cols(x[q], c[q * CAPP:(q + 1) * CAPP]))) for q in range(N)], axis=1)
        far = arrived.reshape(128, -1, 4)[:, entries(slot[r])].reshape(128, -1)
        M.append(mx_ref.quantize(((cols(x[r], entries(own[r])).astype(np.float32) + far) * np.float32(0.5)).astype(BF)))
    y = np.zeros((N, 128, 3 * S), np.float32)
    for r in range(N):
        for i in range(3): y[r][:, S * i:S * i + S] = mx_ref.matmul(mx_ref.quantize(w[r]), M[(r - 1 + i) % N])
    return {"y": y}

from concourse.bass import DstId, RemoteDMATransfer
from concourse.mybir import dt, AluOpType, ActivationFunctionType

CODE = "float8_e4m3fn_x4"
SCRATCH = {
    "wantr": ("sbuf", [128, 24], "int32"),
    "ownr": ("sbuf", [128, 16], "int32"),
    "slotr": ("sbuf", [128, 16], "int32"),
    "req": ("sbuf", [128, 24], "uint16"),
    "selfoff": ("sbuf", [128, 4], "uint16"),
    "landc": ("sbuf", [128, 12], "uint16"),
    "landp": ("sbuf", [128, 12], "uint16"),
    "ownoff": ("sbuf", [128, 16], "uint16"),
    "slotoff": ("sbuf", [128, 16], "uint16"),
    "xs": ("sbuf", [128, 2048], "bfloat16"),
    "ws": ("sbuf", [128, 512], "bfloat16"),
    "hc": ("sbuf", [128, 768], "bfloat16"),
    "hp": ("sbuf", [128, 768], "bfloat16"),
    "qc": ("sbuf", [128, 192], CODE),
    "qcs": ("sbuf", [128, 192], "uint8"),
    "qp": ("sbuf", [128, 192], CODE),
    "qps": ("sbuf", [128, 192], "uint8"),
    "fc": ("sbuf", [128, 192], CODE),
    "fcs": ("sbuf", [128, 192], "uint8"),
    "fp": ("sbuf", [128, 192], CODE),
    "fps": ("sbuf", [128, 192], "uint8"),
    "diff": ("sbuf", [128, 128], "int32"),
    "ez": ("sbuf", [128, 2048], "bfloat16"),
    "eq": ("sbuf", [128, 512], CODE),
    "eqs": ("sbuf", [128, 512], "uint8"),
    "wq": ("sbuf", [128, 128], CODE),
    "wqs": ("sbuf", [128, 128], "uint8"),
    "acol": ("sbuf", [128, 1024], "bfloat16"),
    "fcol": ("sbuf", [128, 1536], "bfloat16"),
    "h": ("sbuf", [128, 1024], "bfloat16"),
    "mq": ("sbuf", [128, 256], CODE),
    "mqs": ("sbuf", [128, 256], "uint8"),
    "onq": ("sbuf", [128, 256], CODE),
    "onqs": ("sbuf", [128, 256], "uint8"),
    "offq": ("sbuf", [128, 256], CODE),
    "offqs": ("sbuf", [128, 256], "uint8"),
    "ysb": ("sbuf", [128, 768], "float32"),
}
for _i in range(8):
    SCRATCH["st%d" % _i] = ("sbuf", [128, 16], "int32")
for _i in range(4):
    SCRATCH["pc%d" % _i] = ("psum", [128, 512], "float32")
    SCRATCH["pp%d" % _i] = ("psum", [128, 512], "float32")

SEMAPHORES = (["ldwant", "ldx", "ldw", "ldown", "ldslot", "iota", "zero", "vreq", "vself", "ve", "veq", "vwq", "lstc", "lstp",
               "vc", "sc", "vp", "sp", "qcd", "qpd", "selfd", "fcd", "fpd", "vown", "va", "sa", "vslot",
               "vf", "sf", "vh0", "vh1", "m0", "m1", "mon", "moff", "mmw", "mmn", "mmf0", "mmf1",
               "yw", "yn", "yf0", "yf1", "stw", "stn", "stf0", "stf1", "loc"]
              + ["mmc%d" % i for i in range(4)] + ["mmp%d" % i for i in range(4)])


def rank_program(g, core, T, topo):
    r = T.rank_of(core)
    if r is None:
        return
    N, CAP, S = 8, 48, 256
    LC = CAP // 16
    A, COPY = AluOpType, ActivationFunctionType.Copy
    V, SC, SY, PE, sem = g.vector, g.scalar, g.sync, g.tensor, T.sem
    cores = T.cores
    chip = [topo.chip(c) for c in cores]

    def groups(q):
        cross = [s for s in range(N) if chip[s] != chip[q] and not topo.same_plane(chip[s], chip[q])]
        return cross, [s for s in range(N) if s not in cross]

    cross, near = groups(r)
    mate = [s for s in near if s != r and chip[s] == chip[r]][0]
    plane = [s for s in near if chip[s] != chip[r]]
    asks = [s for s in near if s != r]
    prv, nxt = (r - 1) % N, (r + 1) % N
    offn = prv if nxt == mate else nxt
    off = topo.engines(core, cores[cross[0]])
    on = [e for e in topo.engines(core, cores[mate]) if e not in off][:4]

    def bits(es):
        return sum(1 << e for e in es)

    def part(i, n):
        k = len(off) // n
        return off[i * k:(i + 1) * k]

    sent = [0]

    def write(d, es, src, dst, rsem):
        rid, pid = topo.addr(cores[d])[:2]
        sent[0] += len(es)
        return RemoteDMATransfer(dst_ids=[DstId(rid=rid, pnc=pid)], dma_engine_mask=bits(es), remote_sem=rsem,
                                 srcs=[src], dsts=[dst])

    def fused(ts):
        g.remote_dma_fused(ts, local_sem=sem.loc)

    def u8(ap):
        return ap.bitcast(dt.uint8)

    for k in range(8):
        (SY if k % 2 == 0 else SC).dma_start(T.wantr[16 * k:16 * k + 16, :], T.want[:]).then_inc(sem.ldwant, 16)
    SY.dma_start(T.xs[:], T.x[:]).then_inc(sem.ldx, 16)
    for k in range(8):
        SY.dma_start(T.ownr[16 * k:16 * k + 16, :], T.own[:]).then_inc(sem.ldown, 16)
    SY.dma_start(T.ws[:], T.w[:]).then_inc(sem.ldw, 16)
    for k in range(8):
        SY.dma_start(T.slotr[16 * k:16 * k + 16, :], T.slot[:]).then_inc(sem.ldslot, 16)

    g.iota(T.diff[:], [[1, 128]], 0, -1).then_inc(sem.iota, 1)
    V.memset(T.ez[:], 0.0).then_inc(sem.zero, 1)
    V.wait_ge(sem.ldwant, 128)
    V.tensor_scalar(T.req[:], T.wantr[:], 4, 0, A.mult, A.max).then_inc(sem.vreq, 1)
    V.tensor_scalar(T.selfoff[:, 0:LC], T.wantr[:, LC * r:LC * r + LC], 4, 0, A.mult, A.max).then_inc(sem.vself, 1)

    def reqs(q):
        return T.req[:, LC * q:LC * q + LC]

    g.wait_ge(sem.vreq, 1)
    ts = []
    for i, q in enumerate(cross):
        k = groups(q)[0].index(r)
        ts.append(write(q, part(i, len(cross)), reqs(q), T.landc[:, LC * k:LC * k + LC], sem.lstc))
    fused(ts)
    ts = []
    for q in plane + [mate]:
        k = [s for s in groups(q)[1] if s != q].index(r)
        es = on if q == mate else part(plane.index(q), len(plane))
        ts.append(write(q, es, reqs(q), T.landp[:, LC * k:LC * k + LC], sem.lstp))
    fused(ts)

    V.wait_ge(sem.iota, 1)
    V.wait_ge(sem.zero, 1)
    for b in range(4):
        V.tensor_scalar(T.ez[:, 512 * b + b:512 * b + 512:4], T.diff[:], 0, 0.5, A.is_equal, A.mult).then_inc(sem.ve, 1)
    V.wait_ge(sem.ve, 4)
    V.quantize_mx(T.eq[:], T.eqs[:], T.ez[:]).then_inc(sem.veq, 1)

    def gather(eng, out, off_ap, t, s):
        src = T.xs[:, t:2048].indirect(off_ap)
        if eng == "v":
            V.tensor_copy(out, src).then_inc(s, 1)
        else:
            SC.activation(out, src, COPY).then_inc(s, 1)

    for eng, q, s in (("v", V, "v"), ("s", SC, "s")):
        tt = (0, 1) if eng == "v" else (2, 3)
        q.wait_ge(sem.vself, 1)
        q.wait_ge(sem.ldx, 16)
        for t in tt:
            gather(eng, T.hp[:, t:4 * CAP:4], T.selfoff[:, 0:LC], t, sem[s + "p"])
        q.wait_ge(sem.lstc, len(off))
        for t in tt:
            gather(eng, T.hc[:, t:768:4], T.landc[:, 0:4 * LC], t, sem[s + "c"])
        if eng == "v":
            V.wait_ge(sem.vc, 2)
            V.wait_ge(sem.sc, 2)
            V.quantize_mx(T.qc[:], T.qcs[:], T.hc[:]).then_inc(sem.qcd, 1)
        q.wait_ge(sem.lstp, len(off) + len(on))
        for t in tt:
            gather(eng, T.hp[:, 4 * CAP + t:768:4], T.landp[:, 0:3 * LC], t, sem[s + "p"])
        if eng == "v":
            V.wait_ge(sem.vp, 4)
            V.wait_ge(sem.sp, 4)
            V.quantize_mx(T.qp[:], T.qps[:], T.hp[:]).then_inc(sem.qpd, 1)

    for w4 in (4, 1):
        if w4 == 4:
            g.wait_ge(sem.qcd, 1)
        ts = []
        for i, q in enumerate(cross):
            k, a = groups(q)[0].index(r), CAP * i
            if w4 == 4:
                src, dst = u8(T.qc[:, a:a + CAP]), u8(T.fc[:, CAP * k:CAP * k + CAP])
            else:
                src, dst = T.qcs[:, a:a + CAP], T.fcs[:, CAP * k:CAP * k + CAP]
            ts.append(write(q, part(i, len(cross)), src, dst, sem.fcd))
        fused(ts)
    for w4 in (4, 1):
        if w4 == 4:
            g.wait_ge(sem.qpd, 1)
        ts = []
        for q in plane + [mate]:
            k, a = groups(q)[1].index(r), CAP * (1 + asks.index(q))
            es = on if q == mate else part(plane.index(q), len(plane))
            if w4 == 4:
                src, dst = u8(T.qp[:, a:a + CAP]), u8(T.fp[:, CAP * k:CAP * k + CAP])
            else:
                src, dst = T.qps[:, a:a + CAP], T.fps[:, CAP * k:CAP * k + CAP]
            ts.append(write(q, es, src, dst, sem.fpd))
        fused(ts)
    ks = CAP * near.index(r)
    SY.wait_ge(sem.qpd, 1)
    SY.dma_start(u8(T.fp[:, ks:ks + CAP]), u8(T.qp[:, 0:CAP])).then_inc(sem.selfd, 16)
    SY.dma_start(T.fps[:, ks:ks + CAP], T.qps[:, 0:CAP]).then_inc(sem.selfd, 16)

    V.wait_ge(sem.ldown, 128)
    V.tensor_scalar(T.ownoff[:], T.ownr[:], 4, None, A.mult).then_inc(sem.vown, 1)
    V.wait_ge(sem.vown, 1)
    SC.wait_ge(sem.vown, 1)
    for t in range(2):
        V.tensor_scalar(T.acol[:, S * t:S * t + S], T.xs[:, t:2048].indirect(T.ownoff[:]), 0.5, None, A.mult).then_inc(sem.va, 1)
    for t in range(2, 4):
        SC.activation(T.acol[:, S * t:S * t + S], T.xs[:, t:2048].indirect(T.ownoff[:]), COPY, scale=0.5).then_inc(sem.sa, 1)

    first, second = (cross, near) if 0 in cross else (near, cross)
    land = first + second
    base = {"c": CAP * land.index(cross[0]), "p": CAP * land.index(near[0])}
    steps, prev = [], 0
    for q in range(1, N):
        d = CAP * (land.index(q) - q)
        if d != prev:
            steps.append((CAP * q, d - prev))
            prev = d
    V.wait_ge(sem.ldslot, 128)
    n = 0
    terms = [T.slotr]
    for j, (at, d) in enumerate(steps):
        V.tensor_scalar(T["st%d" % j][:], T.slotr[:], at, d, A.is_ge, A.mult).then_inc(sem.vslot, 1)
        terms.append(T["st%d" % j])
        n += 1
    fresh = len(steps)
    while len(terms) > 1:
        V.wait_ge(sem.vslot, n)
        nxt_terms = []
        for j in range(0, len(terms) - 1, 2):
            o = T["st%d" % fresh]
            fresh += 1
            V.tensor_tensor(o[:], terms[j][:], terms[j + 1][:], A.add).then_inc(sem.vslot, 1)
            n += 1
            nxt_terms.append(o)
        if len(terms) % 2:
            nxt_terms.append(terms[-1])
        terms = nxt_terms
    V.wait_ge(sem.vslot, n)
    V.tensor_copy(T.slotoff[:], terms[0][:]).then_inc(sem.vslot, 1)
    n += 1
    V.wait_ge(sem.ldw, 16)
    V.quantize_mx(T.wq[:], T.wqs[:], T.ws[:]).then_inc(sem.vwq, 1)

    PE.wait_ge(sem.veq, 1)
    order = (0, 2, 1, 3)
    for c, wide in (("c", 192), ("p", 192)):
        if c == "c":
            PE.wait_ge(sem.fcd, 2 * len(off))
        else:
            PE.wait_ge(sem.selfd, 32)
            PE.wait_ge(sem.fpd, 2 * (len(off) + len(on)))
        codes, scales = (T.fc, T.fcs) if c == "c" else (T.fp, T.fps)
        for b in order:
            PE.matmul_mx(T["p%s%d" % (c, b)][:, 0:wide], T.eq[:, 128 * b:128 * b + 128], T.eqs[:, 128 * b:128 * b + 128],
                         codes[:, 0:wide], scales[:, 0:wide], True, True).then_inc(sem["mm%s%d" % (c, b)], 1)
        for b in range(4):
            o = T.fcol[:, 384 * b + base[c]:384 * b + base[c] + wide]
            src = T["p%s%d" % (c, b)][:, 0:wide]
            if b < 2:
                V.wait_ge(sem["mm%s%d" % (c, b)], 1)
                V.tensor_copy(o, src).then_inc(sem.vf, 1)
            else:
                SC.wait_ge(sem["mm%s%d" % (c, b)], 1)
                SC.activation(o, src, COPY).then_inc(sem.sf, 1)

    V.wait_ge(sem.vslot, n)
    V.wait_ge(sem.va, 2)
    V.wait_ge(sem.sa, 2)
    V.wait_ge(sem.vf, 4)
    for hf in range(2):
        for t in range(4):
            if hf == 0 and t == 2:
                V.wait_ge(sem.sf, 4)
            V.tensor_tensor(T.h[:, 512 * hf + t:512 * hf + 512:4],
                            T.fcol[:, 384 * t:384 * t + 384].indirect(T.slotoff[:, 8 * hf:8 * hf + 8]),
                            T.acol[:, S * t + 128 * hf:S * t + 128 * hf + 128], A.add).then_inc(sem["vh%d" % hf], 1)
        V.wait_ge(sem["vh%d" % hf], 4)
        V.quantize_mx(T.mq[:, 128 * hf:128 * hf + 128], T.mqs[:, 128 * hf:128 * hf + 128],
                      T.h[:, 512 * hf:512 * hf + 512]).then_inc(sem["m%d" % hf], 1)
        g.wait_ge(sem["m%d" % hf], 1)
        a, b = 128 * hf, 128 * hf + 128
        fused([write(offn, off, u8(T.mq[:, a:b]), u8(T.offq[:, a:b]), sem.moff),
               write(mate, on, u8(T.mq[:, a:b]), u8(T.onq[:, a:b]), sem.mon)])
    fused([write(offn, off, T.mqs[:], T.offqs[:], sem.moff), write(mate, on, T.mqs[:], T.onqs[:], sem.mon)])

    sec = {prv: 0, r: 1, nxt: 2}

    def ycols(q, a, b):
        return slice(S * sec[q] + a, S * sec[q] + b)

    PE.wait_ge(sem.vwq, 1)
    PE.wait_ge(sem.m0, 1)
    PE.wait_ge(sem.m1, 1)
    PE.matmul_mx(T.pc0[:, 0:S], T.wq[:], T.wqs[:], T.mq[:], T.mqs[:], True, True).then_inc(sem.mmw, 1)
    PE.wait_ge(sem.mon, 3 * len(on))
    PE.matmul_mx(T.pc1[:, 0:S], T.wq[:], T.wqs[:], T.onq[:], T.onqs[:], True, True).then_inc(sem.mmn, 1)
    PE.wait_ge(sem.moff, 3 * len(off))
    PE.matmul_mx(T.pc2[:, 0:128], T.wq[:], T.wqs[:], T.offq[:, 0:128], T.offqs[:, 0:128], True, True).then_inc(sem.mmf0, 1)
    PE.matmul_mx(T.pc3[:, 0:128], T.wq[:], T.wqs[:], T.offq[:, 128:256], T.offqs[:, 128:256], True, True).then_inc(sem.mmf1, 1)

    V.wait_ge(sem.mmw, 1)
    V.tensor_copy(T.ysb[:, ycols(r, 0, S)], T.pc0[:, 0:S]).then_inc(sem.yw, 1)
    SC.wait_ge(sem.mmn, 1)
    SC.activation(T.ysb[:, ycols(mate, 0, S)], T.pc1[:, 0:S], COPY).then_inc(sem.yn, 1)
    V.wait_ge(sem.mmf0, 1)
    V.tensor_copy(T.ysb[:, ycols(offn, 0, 128)], T.pc2[:, 0:128]).then_inc(sem.yf0, 1)
    SC.wait_ge(sem.mmf1, 1)
    SC.activation(T.ysb[:, ycols(offn, 128, S)], T.pc3[:, 0:128], COPY).then_inc(sem.yf1, 1)

    SY.wait_ge(sem.yw, 1)
    SY.dma_start(T.y[:, ycols(r, 0, S)], T.ysb[:, ycols(r, 0, S)]).then_inc(sem.stw, 16)
    SY.wait_ge(sem.yn, 1)
    SY.dma_start(T.y[:, ycols(mate, 0, S)], T.ysb[:, ycols(mate, 0, S)]).then_inc(sem.stn, 16)
    SY.wait_ge(sem.yf0, 1)
    SY.dma_start(T.y[:, ycols(offn, 0, 128)], T.ysb[:, ycols(offn, 0, 128)]).then_inc(sem.stf0, 16)
    SC.wait_ge(sem.yf1, 1)
    SC.dma_start(T.y[:, ycols(offn, 128, S)], T.ysb[:, ycols(offn, 128, S)]).then_inc(sem.stf1, 16)

    g.wait_ge(sem.loc, sent[0])
    SY.wait_ge(sem.stw, 16)
    SY.wait_ge(sem.stn, 16)
    SY.wait_ge(sem.stf0, 16)
    SC.wait_ge(sem.stf1, 16)
